import numpy as np
import ml_dtypes


def mxq(x, axis, fmt="e4m3"):
    dtype, down = {"e4m3": (ml_dtypes.float8_e4m3fn, 7), "e5m2": (ml_dtypes.float8_e5m2, 14)}[fmt]
    v = np.moveaxis(np.asarray(x, np.float32).astype(ml_dtypes.bfloat16).astype(np.float64), axis, -1)
    blocks = v.reshape(v.shape[:-1] + (-1, 32))
    amax = np.abs(blocks).max(-1, keepdims=True)
    byte = np.maximum(np.where(amax > 0, np.frexp(amax)[1] - 1 + 127, 0) - down, 1)
    scale = np.exp2(byte - 127.0)
    codes = (blocks / scale).astype(np.float32).astype(dtype).astype(np.float64)
    return np.moveaxis((codes * scale).reshape(v.shape), -1, axis)


WIDE = False


def mx_kscale(k):
    if not WIDE:
        return np.ones(k)
    levels = np.array([10, -10, 5, -5, 0])
    if k % 512:
        return np.exp2(np.random.permutation(np.resize(levels, k // 32))).repeat(32)
    a = np.empty((k // 512, 16))
    for p in range(k // 512):
        a[p, :8] = np.random.permutation(np.resize(levels, 8))
        for g in range(8):
            far = levels[np.abs(levels - a[p, g]) >= 10]
            a[p, g + 8] = far[np.random.randint(len(far))]
    return np.exp2(a.ravel()).repeat(32)


def f64(x):
    return np.asarray(x).astype(np.float64)


def striped(idx):
    return np.tile(idx.reshape(-1, 16).T, (8, 1)).astype(np.uint16)


def unstriped(offs):
    return offs[:16].T.reshape(-1).astype(np.int64)


def striped8(idx):
    return np.concatenate([x.reshape(-1, 16).T for x in idx]).astype(np.uint16)


def runs(offs, k):
    lists = np.stack([offs[16 * r : 16 * r + 16].T.reshape(-1) for r in range(8)]).astype(np.int64)
    return lists[np.arange(k) % 512 // 64]


def pack_weight(w):
    k, n = w.shape
    w = f64(np.asarray(w, np.float32).astype(ml_dtypes.bfloat16)).reshape(k // 32, 32, n)
    amax = np.abs(w).max(1)
    byte = np.clip(np.where(amax > 0, np.frexp(amax)[1] - 1 + 127 - 7, 1), 1, 254)
    scaled = (w * np.exp2(127.0 - byte)[:, None, :]).reshape(k, n).astype(np.float32)
    words = np.ascontiguousarray(scaled.reshape(k // 512, 128, 4, n).transpose(0, 1, 3, 2)).astype(ml_dtypes.float8_e4m3fn).view(np.uint8)
    return words, np.ascontiguousarray(byte.astype(np.uint8).reshape(k // 512, 16, n))


def unpack_weight(words, scales):
    g, p, n, _ = words.shape
    vals = np.ascontiguousarray(words).view(ml_dtypes.float8_e4m3fn).astype(np.float64) * np.repeat(np.exp2(scales.astype(np.float64) - 127.0), 8, axis=1)[..., None]
    return vals.transpose(0, 1, 3, 2).reshape(g * 512, n)


E2M1 = np.array([0.0, 0.5, 1.0, 1.5, 2.0, 3.0, 4.0, 6.0, -0.0, -0.5, -1.0, -1.5, -2.0, -3.0, -4.0, -6.0])


def pack_fp4(w):
    k, n = w.shape
    w = f64(np.asarray(w, np.float32).astype(ml_dtypes.bfloat16)).reshape(k // 32, 32, n)
    amax = np.abs(w).max(1)
    mant, ex = np.frexp(amax / 6.0)
    byte = np.clip(np.where(amax > 0, np.where(mant > 0.5, ex, ex - 1) + 127, 1), 1, 254)
    scaled = (w * np.exp2(127.0 - byte)[:, None, :]).reshape(k, n).astype(np.float32)
    c = np.ascontiguousarray(scaled.reshape(k // 512, 128, 4, n).transpose(0, 1, 3, 2)).astype(ml_dtypes.float4_e2m1fn).view(np.uint8) & 0xF
    words = (c[..., 0::2] | (c[..., 1::2] << 4)).reshape(k // 512, 128, 2 * n)
    return np.ascontiguousarray(words), np.ascontiguousarray(byte.astype(np.uint8).reshape(k // 512, 16, n))


def unpack_fp4(words, scales):
    g, _, n = scales.shape
    words = np.ascontiguousarray(words).reshape(g, 128, n, 2)
    nib = np.empty((g, 128, n, 4), np.uint8)
    nib[..., 0::2] = words & 0xF
    nib[..., 1::2] = words >> 4
    vals = E2M1[nib] * np.repeat(np.exp2(scales.astype(np.float64) - 127.0), 8, axis=1)[..., None]
    return vals.transpose(0, 1, 3, 2).reshape(g * 512, n)


def planes(y):
    n, m = y.shape
    v = y.astype(np.float32).astype(ml_dtypes.bfloat16).astype(np.float64).reshape(n // 32, 32, m)
    top = np.abs(v).max(1)
    byte = np.clip(np.where(top > 0, np.frexp(top)[1] - 1 + 127 - 7, 1), 1, 254)
    codes = (v * np.exp2(127.0 - byte)[:, None, :]).reshape(n, m).astype(np.float32).astype(ml_dtypes.float8_e4m3fn).view(np.uint8)
    words = codes.reshape(n // 512, 128, 4, m).transpose(0, 1, 3, 2)
    return np.ascontiguousarray(words), np.ascontiguousarray(byte.astype(np.uint8).reshape(n // 512, 16, m))


K, T, S, N, G, H = 512, 2048, 512, 512, 2048, 512


def setup_inputs():
    n = np.random.standard_normal
    s = mx_kscale(K)[:, None]
    u = mx_kscale(H)
    packed_xT = pack_weight(n((K, T)) * s)
    packed_dT = pack_weight(n((K, G)) / s)
    packed_w1 = pack_fp4(n((H, N)) / np.sqrt(H) / u[:, None])
    return {
        "x_words": packed_xT[0],
        "x_scales": packed_xT[1],
        "d_words": packed_dT[0],
        "d_scales": packed_dT[1],
        "gn": (np.random.uniform(0.5, 1.5, (H, 1)) * u[:, None]).astype(np.float32),
        "w1_words": packed_w1[0],
        "w1_scales": packed_w1[1],
        "offs": striped(np.random.permutation(T)[:S]),
        "kidx": striped8(np.random.randint(0, G, (8, H))),
        "n1": striped8(np.stack([np.random.permutation(S) for _ in range(8)])),
        "n2": striped8(np.stack([np.random.permutation(S) for _ in range(8)])),
    }


def reference(x_words, x_scales, d_words, d_scales, gn, w1_words, w1_scales, offs, kidx, n1, n2):
    d_kidx = unpack_weight(d_words, d_scales)[np.arange(K)[:, None], runs(kidx, K)]
    xq = unpack_weight(x_words, x_scales)[:, unstriped(offs)]
    s = 0.0625 * (d_kidx.T @ xq)
    a = s[np.arange(H)[:, None], runs(n1, H)]
    b = s[np.arange(H)[:, None], runs(n2, H)]
    z = f64(gn) * (np.maximum(np.minimum(s, a), np.minimum(np.maximum(s, a), b)))
    out_0 = unpack_fp4(w1_words, w1_scales).T @ mxq(z, 0, "e4m3")
    return (out_0,) + planes(out_0)

@@ -1,0 +1,263 @@
+from contextlib import ExitStack
+
+import concourse.mybir as mybir
+
+K, T, S, N, G, H = 512, 2048, 512, 512, 2048, 512
+FLOPS = 2 * K * H * S + 2 * H * N * S
+
+F32 = mybir.dt.float32
+BF16 = mybir.dt.bfloat16
+I32 = mybir.dt.int32
+U32 = mybir.dt.uint32
+U16 = mybir.dt.uint16
+U8 = mybir.dt.uint8
+FP8X4 = mybir.dt.float8_e4m3fn_x4
+FP4X4 = mybir.dt.float4_e2m1fn_x4
+MIN = mybir.AluOpType.min
+MAX = mybir.AluOpType.max
+COPY = mybir.ActivationFunctionType.Copy
+
+P = 128
+PACK = 4
+BLOCK = 128
+CHUNKS = (256, 128, 128)
+
+
+def tile_picked_scoremed_none_po_kernel(
+    tc, x_words, x_scales, d_words, d_scales, gn, w1_words, w1_scales, offs, kidx, n1, n2, out_0, out_1, out_2
+):
+    nc = tc.nc
+    with ExitStack() as ctx:
+        lists = ctx.enter_context(tc.tile_pool(name="lists", bufs=1))
+        keep = ctx.enter_context(tc.tile_pool(name="keep", bufs=1))
+        psum = ctx.enter_context(tc.psum_pool(name="psum", bufs=1))
+
+        def sb(name, shape, dtype):
+            return keep.tile(shape, dtype, name=name, align_bytes=64)
+
+        kidx_t = lists.tile([P, H // 16], U16, name="kidx_t")
+        offs_t = lists.tile([P, S // 16], U16, name="offs_t")
+        n1_t = lists.tile([P, S // 16], U16, name="n1_t")
+        n2_t = lists.tile([P, S // 16], U16, name="n2_t")
+        nc.sync.dma_start(kidx_t[:], kidx)
+        nc.sync.dma_start(offs_t[:], offs)
+        nc.sync.dma_start(n1_t[:], n1)
+        nc.sync.dma_start(n2_t[:], n2)
+
+        gn_t = sb("gn_t", [P, PACK], F32)
+        nc.sync.dma_start(gn_t[:], gn.rearrange("(p t) o -> p (t o)", t=PACK))
+
+        ds_table = sb("ds_table", [P, G], U8)
+        xs_table = sb("xs_table", [P, T], U8)
+        ws_raw = sb("ws_raw", [P, N], U8)
+        d_scale = sb("d_scale", [P, H], U8)
+        for plane in (ds_table, xs_table, ws_raw, d_scale):
+            nc.vector.memset(plane[:].bitcast(I32), 0)
+        nc.sync.dma_start(ds_table[0:P:8, :].bitcast(I32), d_scales[0].bitcast(I32))
+        d_table = sb("d_table", [P, G], I32)
+        x_table = sb("x_table", [P, T], I32)
+        nc.sync.dma_start(d_table[:], d_words[0].rearrange("p n t -> p (n t)").bitcast(I32))
+        nc.sync.dma_start(x_table[:], x_words[0].rearrange("p n t -> p (n t)").bitcast(I32))
+        w_raw = sb("w_raw", [P, 2 * N], U8)
+        nc.sync.dma_start(w_raw[:].bitcast(I32), w1_words[0].bitcast(I32))
+        for q in range(4):
+            nc.scalar.dma_start(xs_table[32 * q : 32 * q + 4, :].bitcast(I32), x_scales[0, 4 * q : 4 * q + 4, :].bitcast(I32))
+        for q in range(4):
+            nc.scalar.dma_start(ws_raw[32 * q : 32 * q + 4, :].bitcast(I32), w1_scales[0, 4 * q : 4 * q + 4, :].bitcast(I32))
+
+        gain = sb("gain", [P, PACK], F32)
+        nc.scalar.activation(gain[:], gn_t[:], COPY, scale=0.0625)
+
+        def deal(dst, src, run):
+            nc.vector.tensor_copy(
+                dst.rearrange("p (t c i) -> p c t i", t=PACK, i=run),
+                src.rearrange("p (c i t) -> p c t i", t=PACK, i=run),
+            )
+
+        ds_picked = sb("ds_picked", [P, H], U8)
+        nc.vector.tensor_copy(ds_picked[:], ds_table[:].indirect(kidx_t[:]))
+        ds_dealt = sb("ds_dealt", [P, H], U8)
+        deal(ds_dealt[:], ds_picked[:], 16)
+        for r in range(4):
+            nc.sync.dma_start(d_scale[r:P:32, :].bitcast(I32), ds_dealt[8 * r : P : 32, :].bitcast(I32))
+
+        d_picked = sb("d_picked", [P, H], U32)
+        nc.vector.tensor_copy(d_picked[:], d_table[:].bitcast(U32).indirect(kidx_t[:]))
+        d_code = sb("d_code", [P, H], U32)
+        deal(d_code[:], d_picked[:], 4)
+
+        x_scale = sb("x_scale", [P, S], U8)
+        nc.vector.tensor_copy(x_scale[:], xs_table[:].indirect(offs_t[:]))
+        x_code = sb("x_code", [P, S], U32)
+        half = S // 2
+        for h in range(2):
+            nc.vector.tensor_copy(
+                x_code[:, h * half : (h + 1) * half],
+                x_table[:].bitcast(U32).indirect(offs_t[:, h * half // 16 : (h + 1) * half // 16]),
+            )
+
+        score = [sb("score%d" % t, [P, S], F32) for t in range(PACK)]
+        score_bf = sb("score_bf", [P, PACK, S], BF16)
+
+        def scores(t, cols, bank):
+            keys = slice(t * P, (t + 1) * P)
+            nc.tensor.matmul_mx(
+                out=bank,
+                lhsT=d_code[:, keys].bitcast(FP8X4),
+                lhsT_scale=d_scale[:, keys],
+                rhs=x_code[:, cols].bitcast(FP8X4),
+                rhs_scale=x_scale[:, cols],
+                start=True,
+                stop=True,
+            )
+            nc.scalar.activation(score[t][:, cols], bank, COPY, scale=gain[:, t : t + 1])
+
+        for h in range(2):
+            bank = psum.tile([P, half], F32, name="first%d" % h)
+            scores(0, slice(h * half, (h + 1) * half), bank[:])
+        for t in range(1, PACK):
+            bank = psum.tile([P, S], F32, name="bank%d" % t)
+            scores(t, slice(0, S), bank[:])
+
+        w_code = sb("w_code", [P, 2 * N], U8)
+        nc.vector.tensor_copy(
+            w_code[:].rearrange("p (t c i b) -> p c t i b", t=PACK, i=8, b=2),
+            w_raw[:].rearrange("p (c i t b) -> p c t i b", t=PACK, i=8, b=2),
+        )
+        w_scale = sb("w_scale", [P, N], U8)
+        deal(w_scale[:], ws_raw[:], 16)
+
+        for cols in (slice(0, CHUNKS[0]), slice(CHUNKS[0], S)):
+            for t in range(PACK):
+                nc.scalar.copy(score_bf[:, t, cols], score[t][:, cols])
+
+        z_code = sb("z_code", [P, S], U32)
+        z_scale = sb("z_scale", [P, S], U8)
+        o_code = sb("o_code", [P, S], U32)
+        o_scale = sb("o_scale", [P, S], U8)
+        out_rows = out_0.rearrange("(p t) j -> p t j", t=PACK)
+        out_words = out_1[0].rearrange("p n t -> p (n t)").bitcast(I32)
+
+        starts = [sum(CHUNKS[:c]) for c in range(len(CHUNKS))]
+        last = len(CHUNKS) - 1
+        tiles = {}
+
+        def cols_of(c):
+            return slice(starts[c], starts[c] + CHUNKS[c])
+
+        def tile_of(kind, c, shape, dtype):
+            if (kind, c) not in tiles:
+                tiles[(kind, c)] = sb("%s%d" % (kind, c), shape, dtype)
+            return tiles[(kind, c)]
+
+        def fetch(kind, c, t):
+            n = CHUNKS[c]
+            entries = slice(starts[c] // 16, (starts[c] + n) // 16)
+            dst = tile_of(kind, c, [P, PACK, n], BF16)
+            nc.vector.tensor_copy(dst[:, t, :], score[t][:].indirect((n1_t if kind == "a" else n2_t)[:, entries]))
+
+        def bounds(c):
+            shape = [P, PACK, CHUNKS[c]]
+            s = score_bf[:, :, cols_of(c)]
+            nc.vector.tensor_tensor(tile_of("hi", c, shape, BF16)[:], s, tiles[("a", c)][:], MAX)
+            nc.vector.tensor_tensor(tile_of("lo", c, shape, BF16)[:], s, tiles[("a", c)][:], MIN)
+
+        def cap(c, ts=slice(0, PACK)):
+            hi = tiles[("hi", c)][:, ts, :]
+            nc.vector.tensor_tensor(hi, hi, tiles[("b", c)][:, ts, :], MIN)
+
+        def floor(c, ts=slice(0, PACK)):
+            lo = tiles[("lo", c)][:, ts, :]
+            nc.vector.tensor_tensor(lo, lo, tiles[("hi", c)][:, ts, :], MAX)
+
+        def weave(c):
+            z = tile_of("z", c, [P, CHUNKS[c], PACK], BF16)
+            dst = z[:].rearrange("p (c i) t -> p c t i", i=4)
+            src = tiles[("lo", c)][:].rearrange("p t (c i) -> p c t i", i=4)
+            if c == last:
+                nc.vector.tensor_copy(dst, src)
+            else:
+                nc.scalar.copy(dst, src)
+
+        def quantise(kind, c, codes, scales):
+            cols = cols_of(c)
+            nc.vector.quantize_mx(
+                out=codes[:, cols].bitcast(FP8X4),
+                scales=scales[:, cols],
+                in_=tiles[(kind, c)][:].rearrange("p n t -> p (n t)"),
+            )
+
+        def values(c):
+            n = CHUNKS[c]
+            res = tile_of("res", c, [P, PACK, n], F32)
+            res_bf = tile_of("r", c, [P, n, PACK], BF16)
+            for j0 in range(0, n, BLOCK):
+                cols = slice(starts[c] + j0, starts[c] + j0 + BLOCK)
+                bank = psum.tile([P, PACK, BLOCK], F32, name="bank%d" % (cols.start // BLOCK % 3 + 1))
+                for t in range(PACK):
+                    nc.tensor.matmul_mx(
+                        out=bank[:, t, :],
+                        lhsT=w_code[:, 2 * t * P : 2 * (t + 1) * P].bitcast(FP4X4),
+                        lhsT_scale=w_scale[:, t * P : (t + 1) * P],
+                        rhs=z_code[:, cols].bitcast(FP8X4),
+                        rhs_scale=z_scale[:, cols],
+                        start=True,
+                        stop=True,
+                    )
+                woven = bank[:].rearrange("p t n -> p n t")
+                if c == last:
+                    nc.vector.tensor_copy(res_bf[:, j0 : j0 + BLOCK, :], woven)
+                else:
+                    nc.scalar.copy(res_bf[:, j0 : j0 + BLOCK, :], woven)
+                nc.scalar.copy(res[:, :, j0 : j0 + BLOCK], bank[:])
+            nc.sync.dma_start(out_rows[:, :, cols_of(c)], res[:])
+
+        def planes(c):
+            quantise("r", c, o_code, o_scale)
+            nc.sync.dma_start(out_words[:, cols_of(c)], o_code[:, cols_of(c)].bitcast(I32))
+
+        for t in range(PACK):
+            fetch("a", 0, t)
+            fetch("b", 0, t)
+        fetch("a", 1, 0)
+        bounds(0)
+        fetch("a", 1, 1)
+        cap(0)
+        fetch("a", 1, 2)
+        floor(0)
+        weave(0)
+        fetch("a", 1, 3)
+        fetch("b", 1, 0)
+        bounds(1)
+        fetch("b", 1, 1)
+        fetch("b", 1, 2)
+        fetch("b", 1, 3)
+        quantise("z", 0, z_code, z_scale)
+        values(0)
+        fetch("a", 2, 0)
+        cap(1)
+        fetch("a", 2, 1)
+        floor(1)
+        weave(1)
+        fetch("a", 2, 2)
+        fetch("a", 2, 3)
+        fetch("b", 2, 0)
+        bounds(2)
+        quantise("z", 1, z_code, z_scale)
+        values(1)
+        fetch("b", 2, 1)
+        fetch("b", 2, 2)
+        cap(2, slice(0, 2))
+        fetch("b", 2, 3)
+        floor(2, slice(0, 2))
+        cap(2, slice(2, 4))
+        planes(0)
+        floor(2, slice(2, 4))
+        planes(1)
+        weave(2)
+        quantise("z", 2, z_code, z_scale)
+        values(2)
+        planes(2)
+        for q in range(4):
+            queue = nc.scalar if q % 2 else nc.sync
+            queue.dma_start(out_2[0, 4 * q : 4 * q + 4, :].bitcast(I32), o_scale[32 * q : 32 * q + 4, :].bitcast(I32))

@@ -32,8 +32,8 @@ def tile_picked_scoremed_none_po_kernel(
         keep = ctx.enter_context(tc.tile_pool(name="keep", bufs=1))
         psum = ctx.enter_context(tc.psum_pool(name="psum", bufs=1))
 
-        def sb(name, shape, dtype):
-            return keep.tile(shape, dtype, name=name, align_bytes=64)
+        def sb(name, shape, dtype, tag=""):
+            return keep.tile(shape, dtype, name=name, align_bytes=64, tag=tag or name)
 
         kidx_t = lists.tile([P, H // 16], U16, name="kidx_t")
         offs_t = lists.tile([P, S // 16], U16, name="offs_t")
@@ -46,24 +46,24 @@ def tile_picked_scoremed_none_po_kernel(
 
         gn_t = sb("gn_t", [P, PACK], F32)
         nc.sync.dma_start(gn_t[:], gn.rearrange("(p t) o -> p (t o)", t=PACK))
-
-        ds_table = sb("ds_table", [P, G], U8)
-        xs_table = sb("xs_table", [P, T], U8)
-        ws_raw = sb("ws_raw", [P, N], U8)
-        d_scale = sb("d_scale", [P, H], U8)
-        for plane in (ds_table, xs_table, ws_raw, d_scale):
-            nc.vector.memset(plane[:].bitcast(I32), 0)
-        nc.sync.dma_start(ds_table[0:P:8, :].bitcast(I32), d_scales[0].bitcast(I32))
         d_table = sb("d_table", [P, G], I32)
         x_table = sb("x_table", [P, T], I32)
         nc.sync.dma_start(d_table[:], d_words[0].rearrange("p n t -> p (n t)").bitcast(I32))
         nc.sync.dma_start(x_table[:], x_words[0].rearrange("p n t -> p (n t)").bitcast(I32))
-        w_raw = sb("w_raw", [P, 2 * N], U8)
-        nc.sync.dma_start(w_raw[:].bitcast(I32), w1_words[0].bitcast(I32))
+
+        ds_table = sb("ds_table", [P, G], U8)
+        xs_table = sb("xs_table", [P, T], U8)
+        ws_raw = sb("ws_raw", [P, N], U8)
+        scale = sb("scale", [P, H + S], U8)
+        for table in (ds_table, xs_table):
+            nc.vector.memset(table[:, : G // 2].bitcast(I32), 0)
+            nc.gpsimd.memset(table[:, G // 2 :].bitcast(I32), 0)
+        nc.vector.memset(scale[:].bitcast(I32), 0)
+        nc.gpsimd.memset(ws_raw[:].bitcast(I32), 0)
+        nc.scalar.dma_start(ds_table[0:P:8, :].bitcast(I32), d_scales[0].bitcast(I32))
+        nc.scalar.dma_start(xs_table[0:P:8, :].bitcast(I32), x_scales[0].bitcast(I32))
         for q in range(4):
-            nc.scalar.dma_start(xs_table[32 * q : 32 * q + 4, :].bitcast(I32), x_scales[0, 4 * q : 4 * q + 4, :].bitcast(I32))
-        for q in range(4):
-            nc.scalar.dma_start(ws_raw[32 * q : 32 * q + 4, :].bitcast(I32), w1_scales[0, 4 * q : 4 * q + 4, :].bitcast(I32))
+            nc.gpsimd.dma_start(ws_raw[32 * q : 32 * q + 4, :].bitcast(I32), w1_scales[0, 4 * q : 4 * q + 4, :].bitcast(I32))
 
         gain = sb("gain", [P, PACK], F32)
         nc.scalar.activation(gain[:], gn_t[:], COPY, scale=0.0625)
@@ -76,18 +76,23 @@ def tile_picked_scoremed_none_po_kernel(
 
         ds_picked = sb("ds_picked", [P, H], U8)
         nc.vector.tensor_copy(ds_picked[:], ds_table[:].indirect(kidx_t[:]))
-        ds_dealt = sb("ds_dealt", [P, H], U8)
-        deal(ds_dealt[:], ds_picked[:], 16)
+        spread = sb("spread", [P, H + S], U8)
+        deal(spread[:, :H], ds_picked[:], 16)
+        xs_picked = sb("xs_picked", [P, S], U8)
+        nc.vector.tensor_copy(xs_picked[:], xs_table[:].indirect(offs_t[:]))
+        nc.vector.tensor_copy(spread[:, H:].bitcast(I32), xs_picked[:].bitcast(I32))
         for r in range(4):
-            nc.sync.dma_start(d_scale[r:P:32, :].bitcast(I32), ds_dealt[8 * r : P : 32, :].bitcast(I32))
+            nc.scalar.dma_start(scale[r:P:32, :].bitcast(I32), spread[8 * r : P : 32, :].bitcast(I32))
+        d_scale = scale[:, :H]
+        x_scale = scale[:, H:]
+        w_raw = sb("w_raw", [P, 2 * N], U8, "xs_table")
+        nc.sync.dma_start(w_raw[:].bitcast(I32), w1_words[0].bitcast(I32))
 
         d_picked = sb("d_picked", [P, H], U32)
         nc.vector.tensor_copy(d_picked[:], d_table[:].bitcast(U32).indirect(kidx_t[:]))
         d_code = sb("d_code", [P, H], U32)
         deal(d_code[:], d_picked[:], 4)
 
-        x_scale = sb("x_scale", [P, S], U8)
-        nc.vector.tensor_copy(x_scale[:], xs_table[:].indirect(offs_t[:]))
         x_code = sb("x_code", [P, S], U32)
         half = S // 2
         for h in range(2):
@@ -119,12 +124,12 @@ def tile_picked_scoremed_none_po_kernel(
             bank = psum.tile([P, S], F32, name="bank%d" % t)
             scores(t, slice(0, S), bank[:])
 
-        w_code = sb("w_code", [P, 2 * N], U8)
+        w_code = sb("w_code", [P, 2 * N], U8, "x_table")
         nc.vector.tensor_copy(
             w_code[:].rearrange("p (t c i b) -> p c t i b", t=PACK, i=8, b=2),
             w_raw[:].rearrange("p (c i t b) -> p c t i b", t=PACK, i=8, b=2),
         )
-        w_scale = sb("w_scale", [P, N], U8)
+        w_scale = sb("w_scale", [P, N], U8, "d_table")
         deal(w_scale[:], ws_raw[:], 16)
 
         for cols in (slice(0, CHUNKS[0]), slice(CHUNKS[0], S)):
@@ -147,7 +152,7 @@ def tile_picked_scoremed_none_po_kernel(
 
         def tile_of(kind, c, shape, dtype):
             if (kind, c) not in tiles:
-                tiles[(kind, c)] = sb("%s%d" % (kind, c), shape, dtype)
+                tiles[(kind, c)] = sb("%s%d" % (kind, c), shape, dtype, kind if kind in ("a", "b", "hi") else "")
             return tiles[(kind, c)]
 
         def fetch(kind, c, t):
@@ -172,12 +177,19 @@ def tile_picked_scoremed_none_po_kernel(
 
         def weave(c):
             z = tile_of("z", c, [P, CHUNKS[c], PACK], BF16)
-            dst = z[:].rearrange("p (c i) t -> p c t i", i=4)
-            src = tiles[("lo", c)][:].rearrange("p t (c i) -> p c t i", i=4)
-            if c == last:
-                nc.vector.tensor_copy(dst, src)
-            else:
-                nc.scalar.copy(dst, src)
+            nc.scalar.copy(
+                z[:].rearrange("p (c i) t -> p c t i", i=4),
+                tiles[("lo", c)][:].rearrange("p t (c i) -> p c t i", i=4),
+            )
+
+        def floor_woven(c):
+            z = tile_of("z", c, [P, CHUNKS[c], PACK], BF16)
+            nc.vector.tensor_tensor(
+                z[:].rearrange("p (c i) t -> p c t i", i=8),
+                tiles[("lo", c)][:].rearrange("p t (c i) -> p c t i", i=8),
+                tiles[("hi", c)][:].rearrange("p t (c i) -> p c t i", i=8),
+                MAX,
+            )
 
         def quantise(kind, c, codes, scales):
             cols = cols_of(c)
@@ -187,30 +199,45 @@ def tile_picked_scoremed_none_po_kernel(
                 in_=tiles[(kind, c)][:].rearrange("p n t -> p (n t)"),
             )
 
+        def product(out, t, cols):
+            nc.tensor.matmul_mx(
+                out=out,
+                lhsT=w_code[:, 2 * t * P : 2 * (t + 1) * P].bitcast(FP4X4),
+                lhsT_scale=w_scale[:, t * P : (t + 1) * P],
+                rhs=z_code[:, cols].bitcast(FP8X4),
+                rhs_scale=z_scale[:, cols],
+                start=True,
+                stop=True,
+            )
+
         def values(c):
             n = CHUNKS[c]
             res = tile_of("res", c, [P, PACK, n], F32)
             res_bf = tile_of("r", c, [P, n, PACK], BF16)
             for j0 in range(0, n, BLOCK):
                 cols = slice(starts[c] + j0, starts[c] + j0 + BLOCK)
-                bank = psum.tile([P, PACK, BLOCK], F32, name="bank%d" % (cols.start // BLOCK % 3 + 1))
+                bank = psum.tile([P, PACK, BLOCK], F32, name="bank%d" % (cols.start // BLOCK + 1))
                 for t in range(PACK):
-                    nc.tensor.matmul_mx(
-                        out=bank[:, t, :],
-                        lhsT=w_code[:, 2 * t * P : 2 * (t + 1) * P].bitcast(FP4X4),
-                        lhsT_scale=w_scale[:, t * P : (t + 1) * P],
-                        rhs=z_code[:, cols].bitcast(FP8X4),
-                        rhs_scale=z_scale[:, cols],
-                        start=True,
-                        stop=True,
-                    )
-                woven = bank[:].rearrange("p t n -> p n t")
-                if c == last:
-                    nc.vector.tensor_copy(res_bf[:, j0 : j0 + BLOCK, :], woven)
-                else:
-                    nc.scalar.copy(res_bf[:, j0 : j0 + BLOCK, :], woven)
+                    product(bank[:, t, :], t, cols)
+                nc.scalar.copy(res_bf[:, j0 : j0 + BLOCK, :], bank[:].rearrange("p t n -> p n t"))
                 nc.scalar.copy(res[:, :, j0 : j0 + BLOCK], bank[:])
             nc.sync.dma_start(out_rows[:, :, cols_of(c)], res[:])
+
+        def last_values(c):
+            n = CHUNKS[c]
+            res = tile_of("res", c, [P, PACK, n], F32)
+            res_bf = tile_of("r", c, [P, n, PACK], BF16)
+            for h in range(2):
+                ts = slice(2 * h, 2 * h + 2)
+                bank = psum.tile([P, 2, n], F32, name="first%d" % h)
+                for u in range(2):
+                    product(bank[:, u, :], 2 * h + u, cols_of(c))
+                nc.scalar.copy(res[:, ts, :], bank[:])
+                nc.sync.dma_start(out_rows[:, ts, cols_of(c)], res[:, ts, :])
+            nc.vector.tensor_copy(
+                res_bf[:].rearrange("p (c i) t -> p c t i", i=4),
+                res[:].rearrange("p t (c i) -> p c t i", i=4),
+            )
 
         def planes(c):
             quantise("r", c, o_code, o_scale)
@@ -219,13 +246,13 @@ def tile_picked_scoremed_none_po_kernel(
         for t in range(PACK):
             fetch("a", 0, t)
             fetch("b", 0, t)
-        fetch("a", 1, 0)
         bounds(0)
-        fetch("a", 1, 1)
         cap(0)
-        fetch("a", 1, 2)
+        fetch("a", 1, 0)
         floor(0)
         weave(0)
+        fetch("a", 1, 1)
+        fetch("a", 1, 2)
         fetch("a", 1, 3)
         fetch("b", 1, 0)
         bounds(1)
@@ -247,16 +274,14 @@ def tile_picked_scoremed_none_po_kernel(
         values(1)
         fetch("b", 2, 1)
         fetch("b", 2, 2)
-        cap(2, slice(0, 2))
         fetch("b", 2, 3)
-        floor(2, slice(0, 2))
-        cap(2, slice(2, 4))
+        cap(2, slice(0, 3))
+        cap(2, slice(3, 4))
         planes(0)
-        floor(2, slice(2, 4))
+        floor_woven(2)
         planes(1)
-        weave(2)
         quantise("z", 2, z_code, z_scale)
-        values(2)
+        last_values(2)
         planes(2)
         for q in range(4):
             queue = nc.scalar if q % 2 else nc.sync

@@ -39,31 +39,34 @@ def tile_picked_scoremed_none_po_kernel(
         offs_t = lists.tile([P, S // 16], U16, name="offs_t")
         n1_t = lists.tile([P, S // 16], U16, name="n1_t")
         n2_t = lists.tile([P, S // 16], U16, name="n2_t")
-        nc.sync.dma_start(kidx_t[:], kidx)
-        nc.sync.dma_start(offs_t[:], offs)
-        nc.sync.dma_start(n1_t[:], n1)
-        nc.sync.dma_start(n2_t[:], n2)
-
-        gn_t = sb("gn_t", [P, PACK], F32)
-        nc.sync.dma_start(gn_t[:], gn.rearrange("(p t) o -> p (t o)", t=PACK))
-        d_table = sb("d_table", [P, G], I32)
-        x_table = sb("x_table", [P, T], I32)
-        nc.sync.dma_start(d_table[:], d_words[0].rearrange("p n t -> p (n t)").bitcast(I32))
-        nc.sync.dma_start(x_table[:], x_words[0].rearrange("p n t -> p (n t)").bitcast(I32))
-
         ds_table = sb("ds_table", [P, G], U8)
         xs_table = sb("xs_table", [P, T], U8)
         ws_raw = sb("ws_raw", [P, N], U8)
+        gn_t = sb("gn_t", [P, PACK], F32)
+        d_table = sb("d_table", [P, G], I32)
+        x_table = sb("x_table", [P, T], I32)
+        w_raw = sb("w_raw", [P, 2 * N], U8)
+
+        def load_scales(dst, rows):
+            words = rows.bitcast(I32)
+            nc.sync.dma_start(dst.bitcast(I32), words.unsqueeze(1).to_broadcast([16, 8, words.shape[1]]))
+
+        nc.sync.dma_start(kidx_t[:], kidx)
+        load_scales(ds_table[:], d_scales[0])
+        nc.sync.dma_start(offs_t[:], offs)
+        load_scales(xs_table[:], x_scales[0])
+        load_scales(ws_raw[:], w1_scales[0])
+        nc.sync.dma_start(gn_t[:], gn.rearrange("(p t) o -> p (t o)", t=PACK))
+        nc.sync.dma_start(d_table[:], d_words[0].rearrange("p n t -> p (n t)").bitcast(I32))
+        nc.sync.dma_start(x_table[:], x_words[0].rearrange("p n t -> p (n t)").bitcast(I32))
+        nc.sync.dma_start(w_raw[:].bitcast(I32), w1_words[0].bitcast(I32))
+        nc.sync.dma_start(n1_t[:], n1)
+        nc.sync.dma_start(n2_t[:], n2)
+
         scale = sb("scale", [P, H + S], U8)
-        for table in (ds_table, xs_table):
-            nc.vector.memset(table[:, : G // 2].bitcast(I32), 0)
-            nc.gpsimd.memset(table[:, G // 2 :].bitcast(I32), 0)
+        w_scale = sb("w_scale", [P, N], U8)
         nc.vector.memset(scale[:].bitcast(I32), 0)
-        nc.gpsimd.memset(ws_raw[:].bitcast(I32), 0)
-        nc.scalar.dma_start(ds_table[0:P:8, :].bitcast(I32), d_scales[0].bitcast(I32))
-        nc.scalar.dma_start(xs_table[0:P:8, :].bitcast(I32), x_scales[0].bitcast(I32))
-        for q in range(4):
-            nc.gpsimd.dma_start(ws_raw[32 * q : 32 * q + 4, :].bitcast(I32), w1_scales[0, 4 * q : 4 * q + 4, :].bitcast(I32))
+        nc.vector.memset(w_scale[:].bitcast(I32), 0)
 
         gain = sb("gain", [P, PACK], F32)
         nc.scalar.activation(gain[:], gn_t[:], COPY, scale=0.0625)
@@ -80,13 +83,11 @@ def tile_picked_scoremed_none_po_kernel(
         deal(spread[:, :H], ds_picked[:], 16)
         xs_picked = sb("xs_picked", [P, S], U8)
         nc.vector.tensor_copy(xs_picked[:], xs_table[:].indirect(offs_t[:]))
-        nc.vector.tensor_copy(spread[:, H:].bitcast(I32), xs_picked[:].bitcast(I32))
+        nc.vector.tensor_copy(spread[:, H : H + S].bitcast(I32), xs_picked[:].bitcast(I32))
         for r in range(4):
             nc.scalar.dma_start(scale[r:P:32, :].bitcast(I32), spread[8 * r : P : 32, :].bitcast(I32))
         d_scale = scale[:, :H]
-        x_scale = scale[:, H:]
-        w_raw = sb("w_raw", [P, 2 * N], U8, "xs_table")
-        nc.sync.dma_start(w_raw[:].bitcast(I32), w1_words[0].bitcast(I32))
+        x_scale = scale[:, H : H + S]
 
         d_picked = sb("d_picked", [P, H], U32)
         nc.vector.tensor_copy(d_picked[:], d_table[:].bitcast(U32).indirect(kidx_t[:]))
@@ -124,13 +125,15 @@ def tile_picked_scoremed_none_po_kernel(
             bank = psum.tile([P, S], F32, name="bank%d" % t)
             scores(t, slice(0, S), bank[:])
 
+        ws_dealt = sb("ws_dealt", [P, N], U8, "d_table")
+        deal(ws_dealt[:], ws_raw[:], 16)
+        for r in range(4):
+            nc.sync.dma_start(w_scale[r:P:32, :].bitcast(I32), ws_dealt[8 * r : P : 32, :].bitcast(I32))
         w_code = sb("w_code", [P, 2 * N], U8, "x_table")
         nc.vector.tensor_copy(
             w_code[:].rearrange("p (t c i b) -> p c t i b", t=PACK, i=8, b=2),
             w_raw[:].rearrange("p (c i t b) -> p c t i b", t=PACK, i=8, b=2),
         )
-        w_scale = sb("w_scale", [P, N], U8, "d_table")
-        deal(w_scale[:], ws_raw[:], 16)
 
         for cols in (slice(0, CHUNKS[0]), slice(CHUNKS[0], S)):
             for t in range(PACK):
@@ -177,7 +180,7 @@ def tile_picked_scoremed_none_po_kernel(
 
         def weave(c):
             z = tile_of("z", c, [P, CHUNKS[c], PACK], BF16)
-            nc.scalar.copy(
+            (nc.vector.tensor_copy if c == last else nc.scalar.copy)(
                 z[:].rearrange("p (c i) t -> p c t i", i=4),
                 tiles[("lo", c)][:].rearrange("p t (c i) -> p c t i", i=4),
             )
@@ -274,12 +277,14 @@ def tile_picked_scoremed_none_po_kernel(
         values(1)
         fetch("b", 2, 1)
         fetch("b", 2, 2)
+        cap(2, slice(0, 2))
         fetch("b", 2, 3)
-        cap(2, slice(0, 3))
-        cap(2, slice(3, 4))
+        floor(2, slice(0, 2))
+        cap(2, slice(2, 4))
         planes(0)
-        floor_woven(2)
+        floor(2, slice(2, 4))
         planes(1)
+        weave(2)
         quantise("z", 2, z_code, z_scale)
         last_values(2)
         planes(2)

@@ -19,7 +19,12 @@ COPY = mybir.ActivationFunctionType.Copy
 
 P = 128
 PACK = 4
-BLOCK = 128
+GROUP = 16
+BLOCKS = 16
+BLOCK_P = 8
+QUAD = 32
+LINE = 16
+BANK_COLS = 128
 CHUNKS = (256, 128, 128)
 
 
@@ -35,10 +40,10 @@ def tile_picked_scoremed_none_po_kernel(
         def sb(name, shape, dtype, tag=""):
             return keep.tile(shape, dtype, name=name, align_bytes=64, tag=tag or name)
 
-        kidx_t = lists.tile([P, H // 16], U16, name="kidx_t")
-        offs_t = lists.tile([P, S // 16], U16, name="offs_t")
-        n1_t = lists.tile([P, S // 16], U16, name="n1_t")
-        n2_t = lists.tile([P, S // 16], U16, name="n2_t")
+        kidx_t = lists.tile([P, H // GROUP], U16, name="kidx_t")
+        offs_t = lists.tile([P, S // GROUP], U16, name="offs_t")
+        n1_t = lists.tile([P, S // GROUP], U16, name="n1_t")
+        n2_t = lists.tile([P, S // GROUP], U16, name="n2_t")
         ds_table = sb("ds_table", [P, G], U8)
         xs_table = sb("xs_table", [P, T], U8)
         ws_raw = sb("ws_raw", [P, N], U8)
@@ -49,7 +54,7 @@ def tile_picked_scoremed_none_po_kernel(
 
         def load_scales(dst, rows):
             words = rows.bitcast(I32)
-            nc.sync.dma_start(dst.bitcast(I32), words.unsqueeze(1).to_broadcast([16, 8, words.shape[1]]))
+            nc.sync.dma_start(dst.bitcast(I32), words.unsqueeze(1).to_broadcast([BLOCKS, BLOCK_P, words.shape[1]]))
 
         nc.sync.dma_start(kidx_t[:], kidx)
         load_scales(ds_table[:], d_scales[0])
@@ -63,9 +68,9 @@ def tile_picked_scoremed_none_po_kernel(
         nc.sync.dma_start(n1_t[:], n1)
         nc.sync.dma_start(n2_t[:], n2)
 
-        scale = sb("scale", [P, H + S], U8)
+        dx_scale = sb("dx_scale", [P, H + S], U8)
         w_scale = sb("w_scale", [P, N], U8)
-        nc.vector.memset(scale[:].bitcast(I32), 0)
+        nc.vector.memset(dx_scale[:].bitcast(I32), 0)
         nc.vector.memset(w_scale[:].bitcast(I32), 0)
 
         gain = sb("gain", [P, PACK], F32)
@@ -77,30 +82,31 @@ def tile_picked_scoremed_none_po_kernel(
                 src.rearrange("p (c i t) -> p c t i", t=PACK, i=run),
             )
 
+        def place_rows(queue, dst, src):
+            for r in range(QUAD // BLOCK_P):
+                queue.dma_start(dst[r:P:QUAD, :].bitcast(I32), src[BLOCK_P * r : P : QUAD, :].bitcast(I32))
+
         ds_picked = sb("ds_picked", [P, H], U8)
         nc.vector.tensor_copy(ds_picked[:], ds_table[:].indirect(kidx_t[:]))
-        spread = sb("spread", [P, H + S], U8)
-        deal(spread[:, :H], ds_picked[:], 16)
+        dx_rows = sb("dx_rows", [P, H + S], U8)
+        deal(dx_rows[:, :H], ds_picked[:], LINE)
         xs_picked = sb("xs_picked", [P, S], U8)
         nc.vector.tensor_copy(xs_picked[:], xs_table[:].indirect(offs_t[:]))
-        nc.vector.tensor_copy(spread[:, H : H + S].bitcast(I32), xs_picked[:].bitcast(I32))
-        for r in range(4):
-            nc.scalar.dma_start(scale[r:P:32, :].bitcast(I32), spread[8 * r : P : 32, :].bitcast(I32))
-        d_scale = scale[:, :H]
-        x_scale = scale[:, H : H + S]
+        nc.vector.tensor_copy(dx_rows[:, H:].bitcast(I32), xs_picked[:].bitcast(I32))
+        place_rows(nc.scalar, dx_scale, dx_rows)
+        d_scale = dx_scale[:, :H]
+        x_scale = dx_scale[:, H:]
 
         d_picked = sb("d_picked", [P, H], U32)
         nc.vector.tensor_copy(d_picked[:], d_table[:].bitcast(U32).indirect(kidx_t[:]))
         d_code = sb("d_code", [P, H], U32)
-        deal(d_code[:], d_picked[:], 4)
+        deal(d_code[:], d_picked[:], LINE // 4)
 
         x_code = sb("x_code", [P, S], U32)
-        half = S // 2
-        for h in range(2):
-            nc.vector.tensor_copy(
-                x_code[:, h * half : (h + 1) * half],
-                x_table[:].bitcast(U32).indirect(offs_t[:, h * half // 16 : (h + 1) * half // 16]),
-            )
+        halves = (slice(0, S // 2), slice(S // 2, S))
+        for cols in halves:
+            entries = slice(cols.start // GROUP, cols.stop // GROUP)
+            nc.vector.tensor_copy(x_code[:, cols], x_table[:].bitcast(U32).indirect(offs_t[:, entries]))
 
         score = [sb("score%d" % t, [P, S], F32) for t in range(PACK)]
         score_bf = sb("score_bf", [P, PACK, S], BF16)
@@ -118,21 +124,20 @@ def tile_picked_scoremed_none_po_kernel(
             )
             nc.scalar.activation(score[t][:, cols], bank, COPY, scale=gain[:, t : t + 1])
 
-        for h in range(2):
-            bank = psum.tile([P, half], F32, name="first%d" % h)
-            scores(0, slice(h * half, (h + 1) * half), bank[:])
+        for h, cols in enumerate(halves):
+            bank = psum.tile([P, S // 2], F32, name="half%d" % h)
+            scores(0, cols, bank[:])
         for t in range(1, PACK):
             bank = psum.tile([P, S], F32, name="bank%d" % t)
             scores(t, slice(0, S), bank[:])
 
-        ws_dealt = sb("ws_dealt", [P, N], U8, "d_table")
-        deal(ws_dealt[:], ws_raw[:], 16)
-        for r in range(4):
-            nc.sync.dma_start(w_scale[r:P:32, :].bitcast(I32), ws_dealt[8 * r : P : 32, :].bitcast(I32))
+        ws_rows = sb("ws_rows", [P, N], U8, "d_table")
+        deal(ws_rows[:], ws_raw[:], LINE)
+        place_rows(nc.sync, w_scale, ws_rows)
         w_code = sb("w_code", [P, 2 * N], U8, "x_table")
         nc.vector.tensor_copy(
-            w_code[:].rearrange("p (t c i b) -> p c t i b", t=PACK, i=8, b=2),
-            w_raw[:].rearrange("p (c i t b) -> p c t i b", t=PACK, i=8, b=2),
+            w_code[:].rearrange("p (t c i b) -> p c t i b", t=PACK, i=LINE // 2, b=2),
+            w_raw[:].rearrange("p (c i t b) -> p c t i b", t=PACK, i=LINE // 2, b=2),
         )
 
         for cols in (slice(0, CHUNKS[0]), slice(CHUNKS[0], S)):
@@ -146,12 +151,9 @@ def tile_picked_scoremed_none_po_kernel(
         out_rows = out_0.rearrange("(p t) j -> p t j", t=PACK)
         out_words = out_1[0].rearrange("p n t -> p (n t)").bitcast(I32)
 
-        starts = [sum(CHUNKS[:c]) for c in range(len(CHUNKS))]
         last = len(CHUNKS) - 1
+        chunk_cols = [slice(sum(CHUNKS[:c]), sum(CHUNKS[: c + 1])) for c in range(len(CHUNKS))]
         tiles = {}
-
-        def cols_of(c):
-            return slice(starts[c], starts[c] + CHUNKS[c])
 
         def tile_of(kind, c, shape, dtype):
             if (kind, c) not in tiles:
@@ -159,14 +161,13 @@ def tile_picked_scoremed_none_po_kernel(
             return tiles[(kind, c)]
 
         def fetch(kind, c, t):
-            n = CHUNKS[c]
-            entries = slice(starts[c] // 16, (starts[c] + n) // 16)
-            dst = tile_of(kind, c, [P, PACK, n], BF16)
+            entries = slice(chunk_cols[c].start // GROUP, chunk_cols[c].stop // GROUP)
+            dst = tile_of(kind, c, [P, PACK, CHUNKS[c]], BF16)
             nc.vector.tensor_copy(dst[:, t, :], score[t][:].indirect((n1_t if kind == "a" else n2_t)[:, entries]))
 
         def bounds(c):
             shape = [P, PACK, CHUNKS[c]]
-            s = score_bf[:, :, cols_of(c)]
+            s = score_bf[:, :, chunk_cols[c]]
             nc.vector.tensor_tensor(tile_of("hi", c, shape, BF16)[:], s, tiles[("a", c)][:], MAX)
             nc.vector.tensor_tensor(tile_of("lo", c, shape, BF16)[:], s, tiles[("a", c)][:], MIN)
 
@@ -174,31 +175,20 @@ def tile_picked_scoremed_none_po_kernel(
             hi = tiles[("hi", c)][:, ts, :]
             nc.vector.tensor_tensor(hi, hi, tiles[("b", c)][:, ts, :], MIN)
 
-        def floor(c, ts=slice(0, PACK)):
+        def choose(c, ts=slice(0, PACK)):
             lo = tiles[("lo", c)][:, ts, :]
             nc.vector.tensor_tensor(lo, lo, tiles[("hi", c)][:, ts, :], MAX)
 
-        def weave(c):
-            z = tile_of("z", c, [P, CHUNKS[c], PACK], BF16)
-            (nc.vector.tensor_copy if c == last else nc.scalar.copy)(
-                z[:].rearrange("p (c i) t -> p c t i", i=4),
-                tiles[("lo", c)][:].rearrange("p t (c i) -> p c t i", i=4),
-            )
+        def weave(copy, dst, src):
+            copy(dst.rearrange("p (c i) t -> p c t i", i=4), src.rearrange("p t (c i) -> p c t i", i=4))
 
-        def floor_woven(c):
-            z = tile_of("z", c, [P, CHUNKS[c], PACK], BF16)
-            nc.vector.tensor_tensor(
-                z[:].rearrange("p (c i) t -> p c t i", i=8),
-                tiles[("lo", c)][:].rearrange("p t (c i) -> p c t i", i=8),
-                tiles[("hi", c)][:].rearrange("p t (c i) -> p c t i", i=8),
-                MAX,
-            )
+        def weave_z(c, copy):
+            weave(copy, tile_of("z", c, [P, CHUNKS[c], PACK], BF16)[:], tiles[("lo", c)][:])
 
         def quantise(kind, c, codes, scales):
-            cols = cols_of(c)
             nc.vector.quantize_mx(
-                out=codes[:, cols].bitcast(FP8X4),
-                scales=scales[:, cols],
+                out=codes[:, chunk_cols[c]].bitcast(FP8X4),
+                scales=scales[:, chunk_cols[c]],
                 in_=tiles[(kind, c)][:].rearrange("p n t -> p (n t)"),
             )
 
@@ -216,78 +206,62 @@ def tile_picked_scoremed_none_po_kernel(
         def values(c):
             n = CHUNKS[c]
             res = tile_of("res", c, [P, PACK, n], F32)
-            res_bf = tile_of("r", c, [P, n, PACK], BF16)
-            for j0 in range(0, n, BLOCK):
-                cols = slice(starts[c] + j0, starts[c] + j0 + BLOCK)
-                bank = psum.tile([P, PACK, BLOCK], F32, name="bank%d" % (cols.start // BLOCK + 1))
+            res_bf = tile_of("res_bf", c, [P, n, PACK], BF16)
+            for j0 in range(0, n, BANK_COLS):
+                cols = slice(chunk_cols[c].start + j0, chunk_cols[c].start + j0 + BANK_COLS)
+                bank = psum.tile([P, PACK, BANK_COLS], F32, name="bank%d" % (cols.start // BANK_COLS + 1))
                 for t in range(PACK):
                     product(bank[:, t, :], t, cols)
-                nc.scalar.copy(res_bf[:, j0 : j0 + BLOCK, :], bank[:].rearrange("p t n -> p n t"))
-                nc.scalar.copy(res[:, :, j0 : j0 + BLOCK], bank[:])
-            nc.sync.dma_start(out_rows[:, :, cols_of(c)], res[:])
+                nc.scalar.copy(res_bf[:, j0 : j0 + BANK_COLS, :], bank[:].rearrange("p t n -> p n t"))
+                nc.scalar.copy(res[:, :, j0 : j0 + BANK_COLS], bank[:])
+            nc.sync.dma_start(out_rows[:, :, chunk_cols[c]], res[:])
 
         def last_values(c):
             n = CHUNKS[c]
             res = tile_of("res", c, [P, PACK, n], F32)
-            res_bf = tile_of("r", c, [P, n, PACK], BF16)
+            res_bf = tile_of("res_bf", c, [P, n, PACK], BF16)
             for h in range(2):
-                ts = slice(2 * h, 2 * h + 2)
-                bank = psum.tile([P, 2, n], F32, name="first%d" % h)
+                bank = psum.tile([P, 2, n], F32, name="half%d" % h)
                 for u in range(2):
-                    product(bank[:, u, :], 2 * h + u, cols_of(c))
-                nc.scalar.copy(res[:, ts, :], bank[:])
-                nc.sync.dma_start(out_rows[:, ts, cols_of(c)], res[:, ts, :])
-            nc.vector.tensor_copy(
-                res_bf[:].rearrange("p (c i) t -> p c t i", i=4),
-                res[:].rearrange("p t (c i) -> p c t i", i=4),
-            )
+                    product(bank[:, u, :], 2 * h + u, chunk_cols[c])
+                nc.scalar.copy(res[:, 2 * h : 2 * h + 2, :], bank[:])
+            nc.sync.dma_start(out_rows[:, :, chunk_cols[c]], res[:])
+            weave(nc.vector.tensor_copy, res_bf[:], res[:])
 
-        def planes(c):
-            quantise("r", c, o_code, o_scale)
-            nc.sync.dma_start(out_words[:, cols_of(c)], o_code[:, cols_of(c)].bitcast(I32))
+        def store_words(cols):
+            nc.sync.dma_start(out_words[:, cols], o_code[:, cols].bitcast(I32))
 
         for t in range(PACK):
             fetch("a", 0, t)
             fetch("b", 0, t)
         bounds(0)
-        cap(0)
-        fetch("a", 1, 0)
-        floor(0)
-        weave(0)
-        fetch("a", 1, 1)
-        fetch("a", 1, 2)
-        fetch("a", 1, 3)
-        fetch("b", 1, 0)
-        bounds(1)
-        fetch("b", 1, 1)
-        fetch("b", 1, 2)
-        fetch("b", 1, 3)
-        quantise("z", 0, z_code, z_scale)
-        values(0)
-        fetch("a", 2, 0)
-        cap(1)
-        fetch("a", 2, 1)
-        floor(1)
-        weave(1)
-        fetch("a", 2, 2)
-        fetch("a", 2, 3)
-        fetch("b", 2, 0)
-        bounds(2)
-        quantise("z", 1, z_code, z_scale)
-        values(1)
-        fetch("b", 2, 1)
-        fetch("b", 2, 2)
-        cap(2, slice(0, 2))
-        fetch("b", 2, 3)
-        floor(2, slice(0, 2))
-        cap(2, slice(2, 4))
-        planes(0)
-        floor(2, slice(2, 4))
-        planes(1)
-        weave(2)
-        quantise("z", 2, z_code, z_scale)
-        last_values(2)
-        planes(2)
-        for q in range(4):
+        for c in range(1, len(CHUNKS)):
+            fetch("a", c, 0)
+            cap(c - 1)
+            fetch("a", c, 1)
+            choose(c - 1)
+            weave_z(c - 1, nc.scalar.copy)
+            fetch("a", c, 2)
+            fetch("a", c, 3)
+            fetch("b", c, 0)
+            bounds(c)
+            quantise("z", c - 1, z_code, z_scale)
+            values(c - 1)
+            for t in range(1, PACK):
+                fetch("b", c, t)
+        early, late = slice(0, PACK - 1), slice(PACK - 1, PACK)
+        cap(last, early)
+        cap(last, late)
+        choose(last, early)
+        choose(last, late)
+        weave_z(last, nc.vector.tensor_copy)
+        quantise("z", last, z_code, z_scale)
+        last_values(last)
+        for c in range(len(CHUNKS)):
+            quantise("res_bf", c, o_code, o_scale)
+        store_words(slice(0, chunk_cols[last].start))
+        store_words(chunk_cols[last])
+        for q in range(P // QUAD):
             queue = nc.scalar if q % 2 else nc.sync
-            queue.dma_start(out_2[0, 4 * q : 4 * q + 4, :].bitcast(I32), o_scale[32 * q : 32 * q + 4, :].bitcast(I32))
+            rows = slice(QUAD // BLOCK_P * q, QUAD // BLOCK_P * (q + 1))
+            queue.dma_start(out_2[0, rows, :].bitcast(I32), o_scale[QUAD * q : QUAD * q + 4, :].bitcast(I32))

from contextlib import ExitStack

import concourse.mybir as mybir

K, T, S, N, G, H = 512, 2048, 512, 512, 2048, 512
FLOPS = 2 * K * H * S + 2 * H * N * S

F32 = mybir.dt.float32
BF16 = mybir.dt.bfloat16
I32 = mybir.dt.int32
U32 = mybir.dt.uint32
U16 = mybir.dt.uint16
U8 = mybir.dt.uint8
FP8X4 = mybir.dt.float8_e4m3fn_x4
FP4X4 = mybir.dt.float4_e2m1fn_x4
MIN = mybir.AluOpType.min
MAX = mybir.AluOpType.max
COPY = mybir.ActivationFunctionType.Copy

P = 128
PACK = 4
GROUP = 16
BLOCKS = 16
BLOCK_P = 8
QUAD = 32
LINE = 16
BANK_COLS = 128
CHUNKS = (256, 128, 128)


def tile_picked_scoremed_none_po_kernel(
    tc, x_words, x_scales, d_words, d_scales, gn, w1_words, w1_scales, offs, kidx, n1, n2, out_0, out_1, out_2
):
    nc = tc.nc
    with ExitStack() as ctx:
        lists = ctx.enter_context(tc.tile_pool(name="lists", bufs=1))
        keep = ctx.enter_context(tc.tile_pool(name="keep", bufs=1))
        psum = ctx.enter_context(tc.psum_pool(name="psum", bufs=1))

        def sb(name, shape, dtype, tag=""):
            return keep.tile(shape, dtype, name=name, align_bytes=64, tag=tag or name)

        kidx_t = lists.tile([P, H // GROUP], U16, name="kidx_t")
        offs_t = lists.tile([P, S // GROUP], U16, name="offs_t")
        n1_t = lists.tile([P, S // GROUP], U16, name="n1_t")
        n2_t = lists.tile([P, S // GROUP], U16, name="n2_t")
        ds_table = sb("ds_table", [P, G], U8)
        xs_table = sb("xs_table", [P, T], U8)
        ws_raw = sb("ws_raw", [P, N], U8)
        gn_t = sb("gn_t", [P, PACK], F32)
        d_table = sb("d_table", [P, G], I32)
        x_table = sb("x_table", [P, T], I32)
        w_raw = sb("w_raw", [P, 2 * N], U8)

        def load_scales(dst, rows):
            words = rows.bitcast(I32)
            nc.sync.dma_start(dst.bitcast(I32), words.unsqueeze(1).to_broadcast([BLOCKS, BLOCK_P, words.shape[1]]))

        nc.sync.dma_start(kidx_t[:], kidx)
        load_scales(ds_table[:], d_scales[0])
        nc.sync.dma_start(offs_t[:], offs)
        load_scales(xs_table[:], x_scales[0])
        load_scales(ws_raw[:], w1_scales[0])
        nc.sync.dma_start(gn_t[:], gn.rearrange("(p t) o -> p (t o)", t=PACK))
        nc.sync.dma_start(d_table[:], d_words[0].rearrange("p n t -> p (n t)").bitcast(I32))
        nc.sync.dma_start(x_table[:], x_words[0].rearrange("p n t -> p (n t)").bitcast(I32))
        nc.sync.dma_start(w_raw[:].bitcast(I32), w1_words[0].bitcast(I32))
        nc.sync.dma_start(n1_t[:], n1)
        nc.sync.dma_start(n2_t[:], n2)

        dx_scale = sb("dx_scale", [P, H + S], U8)
        w_scale = sb("w_scale", [P, N], U8)
        nc.vector.memset(dx_scale[:].bitcast(I32), 0)
        nc.vector.memset(w_scale[:].bitcast(I32), 0)

        gain = sb("gain", [P, PACK], F32)
        nc.scalar.activation(gain[:], gn_t[:], COPY, scale=0.0625)

        def deal(dst, src, run):
            nc.vector.tensor_copy(
                dst.rearrange("p (t c i) -> p c t i", t=PACK, i=run),
                src.rearrange("p (c i t) -> p c t i", t=PACK, i=run),
            )

        def place_rows(queue, dst, src):
            for r in range(QUAD // BLOCK_P):
                queue.dma_start(dst[r:P:QUAD, :].bitcast(I32), src[BLOCK_P * r : P : QUAD, :].bitcast(I32))

        ds_picked = sb("ds_picked", [P, H], U8)
        nc.vector.tensor_copy(ds_picked[:], ds_table[:].indirect(kidx_t[:]))
        dx_rows = sb("dx_rows", [P, H + S], U8)
        deal(dx_rows[:, :H], ds_picked[:], LINE)
        xs_picked = sb("xs_picked", [P, S], U8)
        nc.vector.tensor_copy(xs_picked[:], xs_table[:].indirect(offs_t[:]))
        nc.vector.tensor_copy(dx_rows[:, H:].bitcast(I32), xs_picked[:].bitcast(I32))
        place_rows(nc.scalar, dx_scale, dx_rows)
        d_scale = dx_scale[:, :H]
        x_scale = dx_scale[:, H:]

        d_picked = sb("d_picked", [P, H], U32)
        nc.vector.tensor_copy(d_picked[:], d_table[:].bitcast(U32).indirect(kidx_t[:]))
        d_code = sb("d_code", [P, H], U32)
        deal(d_code[:], d_picked[:], LINE // 4)

        x_code = sb("x_code", [P, S], U32)
        halves = (slice(0, S // 2), slice(S // 2, S))
        for cols in halves:
            entries = slice(cols.start // GROUP, cols.stop // GROUP)
            nc.vector.tensor_copy(x_code[:, cols], x_table[:].bitcast(U32).indirect(offs_t[:, entries]))

        score = [sb("score%d" % t, [P, S], F32) for t in range(PACK)]
        score_bf = sb("score_bf", [P, PACK, S], BF16)

        def scores(t, cols, bank):
            keys = slice(t * P, (t + 1) * P)
            nc.tensor.matmul_mx(
                out=bank,
                lhsT=d_code[:, keys].bitcast(FP8X4),
                lhsT_scale=d_scale[:, keys],
                rhs=x_code[:, cols].bitcast(FP8X4),
                rhs_scale=x_scale[:, cols],
                start=True,
                stop=True,
            )
            nc.scalar.activation(score[t][:, cols], bank, COPY, scale=gain[:, t : t + 1])

        for h, cols in enumerate(halves):
            bank = psum.tile([P, S // 2], F32, name="half%d" % h)
            scores(0, cols, bank[:])
        for t in range(1, PACK):
            bank = psum.tile([P, S], F32, name="bank%d" % t)
            scores(t, slice(0, S), bank[:])

        ws_rows = sb("ws_rows", [P, N], U8, "d_table")
        deal(ws_rows[:], ws_raw[:], LINE)
        place_rows(nc.sync, w_scale, ws_rows)
        w_code = sb("w_code", [P, 2 * N], U8, "x_table")
        nc.vector.tensor_copy(
            w_code[:].rearrange("p (t c i b) -> p c t i b", t=PACK, i=LINE // 2, b=2),
            w_raw[:].rearrange("p (c i t b) -> p c t i b", t=PACK, i=LINE // 2, b=2),
        )

        for cols in (slice(0, CHUNKS[0]), slice(CHUNKS[0], S)):
            for t in range(PACK):
                nc.scalar.copy(score_bf[:, t, cols], score[t][:, cols])

        z_code = sb("z_code", [P, S], U32)
        z_scale = sb("z_scale", [P, S], U8)
        o_code = sb("o_code", [P, S], U32)
        o_scale = sb("o_scale", [P, S], U8)
        out_rows = out_0.rearrange("(p t) j -> p t j", t=PACK)
        out_words = out_1[0].rearrange("p n t -> p (n t)").bitcast(I32)

        last = len(CHUNKS) - 1
        chunk_cols = [slice(sum(CHUNKS[:c]), sum(CHUNKS[: c + 1])) for c in range(len(CHUNKS))]
        tiles = {}

        def tile_of(kind, c, shape, dtype):
            if (kind, c) not in tiles:
                tiles[(kind, c)] = sb("%s%d" % (kind, c), shape, dtype, kind if kind in ("a", "b", "hi") else "")
            return tiles[(kind, c)]

        def fetch(kind, c, t):
            entries = slice(chunk_cols[c].start // GROUP, chunk_cols[c].stop // GROUP)
            dst = tile_of(kind, c, [P, PACK, CHUNKS[c]], BF16)
            nc.vector.tensor_copy(dst[:, t, :], score[t][:].indirect((n1_t if kind == "a" else n2_t)[:, entries]))

        def bounds(c):
            shape = [P, PACK, CHUNKS[c]]
            s = score_bf[:, :, chunk_cols[c]]
            nc.vector.tensor_tensor(tile_of("hi", c, shape, BF16)[:], s, tiles[("a", c)][:], MAX)
            nc.vector.tensor_tensor(tile_of("lo", c, shape, BF16)[:], s, tiles[("a", c)][:], MIN)

        def cap(c, ts=slice(0, PACK)):
            hi = tiles[("hi", c)][:, ts, :]
            nc.vector.tensor_tensor(hi, hi, tiles[("b", c)][:, ts, :], MIN)

        def choose(c, ts=slice(0, PACK)):
            lo = tiles[("lo", c)][:, ts, :]
            nc.vector.tensor_tensor(lo, lo, tiles[("hi", c)][:, ts, :], MAX)

        def weave(copy, dst, src):
            copy(dst.rearrange("p (c i) t -> p c t i", i=4), src.rearrange("p t (c i) -> p c t i", i=4))

        def weave_z(c, copy):
            weave(copy, tile_of("z", c, [P, CHUNKS[c], PACK], BF16)[:], tiles[("lo", c)][:])

        def quantise(kind, c, codes, scales):
            nc.vector.quantize_mx(
                out=codes[:, chunk_cols[c]].bitcast(FP8X4),
                scales=scales[:, chunk_cols[c]],
                in_=tiles[(kind, c)][:].rearrange("p n t -> p (n t)"),
            )

        def product(out, t, cols):
            nc.tensor.matmul_mx(
                out=out,
                lhsT=w_code[:, 2 * t * P : 2 * (t + 1) * P].bitcast(FP4X4),
                lhsT_scale=w_scale[:, t * P : (t + 1) * P],
                rhs=z_code[:, cols].bitcast(FP8X4),
                rhs_scale=z_scale[:, cols],
                start=True,
                stop=True,
            )

        def values(c):
            n = CHUNKS[c]
            res = tile_of("res", c, [P, PACK, n], F32)
            res_bf = tile_of("res_bf", c, [P, n, PACK], BF16)
            for j0 in range(0, n, BANK_COLS):
                cols = slice(chunk_cols[c].start + j0, chunk_cols[c].start + j0 + BANK_COLS)
                bank = psum.tile([P, PACK, BANK_COLS], F32, name="bank%d" % (cols.start // BANK_COLS + 1))
                for t in range(PACK):
                    product(bank[:, t, :], t, cols)
                nc.scalar.copy(res_bf[:, j0 : j0 + BANK_COLS, :], bank[:].rearrange("p t n -> p n t"))
                nc.scalar.copy(res[:, :, j0 : j0 + BANK_COLS], bank[:])
            nc.sync.dma_start(out_rows[:, :, chunk_cols[c]], res[:])

        def last_values(c):
            n = CHUNKS[c]
            res = tile_of("res", c, [P, PACK, n], F32)
            res_bf = tile_of("res_bf", c, [P, n, PACK], BF16)
            for h in range(2):
                bank = psum.tile([P, 2, n], F32, name="half%d" % h)
                for u in range(2):
                    product(bank[:, u, :], 2 * h + u, chunk_cols[c])
                nc.scalar.copy(res[:, 2 * h : 2 * h + 2, :], bank[:])
            nc.sync.dma_start(out_rows[:, :, chunk_cols[c]], res[:])
            weave(nc.vector.tensor_copy, res_bf[:], res[:])

        def store_words(cols):
            nc.sync.dma_start(out_words[:, cols], o_code[:, cols].bitcast(I32))

        for t in range(PACK):
            fetch("a", 0, t)
            fetch("b", 0, t)
        bounds(0)
        for c in range(1, len(CHUNKS)):
            fetch("a", c, 0)
            cap(c - 1)
            fetch("a", c, 1)
            choose(c - 1)
            weave_z(c - 1, nc.scalar.copy)
            fetch("a", c, 2)
            fetch("a", c, 3)
            fetch("b", c, 0)
            bounds(c)
            quantise("z", c - 1, z_code, z_scale)
            values(c - 1)
            for t in range(1, PACK):
                fetch("b", c, t)
        early, late = slice(0, PACK - 1), slice(PACK - 1, PACK)
        cap(last, early)
        cap(last, late)
        choose(last, early)
        choose(last, late)
        weave_z(last, nc.vector.tensor_copy)
        quantise("z", last, z_code, z_scale)
        last_values(last)
        for c in range(len(CHUNKS)):
            quantise("res_bf", c, o_code, o_scale)
        store_words(slice(0, chunk_cols[last].start))
        store_words(chunk_cols[last])
        for q in range(P // QUAD):
            queue = nc.scalar if q % 2 else nc.sync
            rows = slice(QUAD // BLOCK_P * q, QUAD // BLOCK_P * (q + 1))
            queue.dma_start(out_2[0, rows, :].bitcast(I32), o_scale[QUAD * q : QUAD * q + 4, :].bitcast(I32))
